import numpy as np
import ml_dtypes


def mxq(x, axis, fmt="e4m3"):
    dtype, down = {"e4m3": (ml_dtypes.float8_e4m3fn, 7), "e5m2": (ml_dtypes.float8_e5m2, 14)}[fmt]
    v = np.moveaxis(np.asarray(x, np.float32).astype(ml_dtypes.bfloat16).astype(np.float64), axis, -1)
    blocks = v.reshape(v.shape[:-1] + (-1, 32))
    amax = np.abs(blocks).max(-1, keepdims=True)
    byte = np.maximum(np.where(amax > 0, np.frexp(amax)[1] - 1 + 127, 0) - down, 1)
    scale = np.exp2(byte - 127.0)
    codes = (blocks / scale).astype(np.float32).astype(dtype).astype(np.float64)
    return np.moveaxis((codes * scale).reshape(v.shape), -1, axis)


WIDE = False


def mx_kscale(k):
    if not WIDE:
        return np.ones(k)
    levels = np.array([10, -10, 5, -5, 0])
    if k % 512:
        return np.exp2(np.random.permutation(np.resize(levels, k // 32))).repeat(32)
    a = np.empty((k // 512, 16))
    for p in range(k // 512):
        a[p, :8] = np.random.permutation(np.resize(levels, 8))
        for g in range(8):
            far = levels[np.abs(levels - a[p, g]) >= 10]
            a[p, g + 8] = far[np.random.randint(len(far))]
    return np.exp2(a.ravel()).repeat(32)


def f64(x):
    return np.asarray(x).astype(np.float64)


def striped(idx):
    return np.tile(np.asarray(idx).reshape(-1, 16).T, (8, 1)).astype(np.uint16)


def unstriped(offs):
    return offs[:16].T.reshape(-1).astype(np.int64)


E2M1 = np.array([0.0, 0.5, 1.0, 1.5, 2.0, 3.0, 4.0, 6.0, -0.0, -0.5, -1.0, -1.5, -2.0, -3.0, -4.0, -6.0])


def pack_weight(w, fmt):
    k, n = w.shape
    w = f64(np.asarray(w, np.float32).astype(ml_dtypes.bfloat16)).reshape(k // 32, 32, n)
    amax = np.abs(w).max(1)
    if fmt == "e4m3":
        byte = np.frexp(amax)[1] - 1 + 127 - 7
    else:
        mant, ex = np.frexp(amax / 6.0)
        byte = np.where(mant > 0.5, ex, ex - 1) + 127
    byte = np.clip(np.where(amax > 0, byte, 1), 1, 254)
    scaled = (w * np.exp2(127.0 - byte)[:, None, :]).reshape(k, n).astype(np.float32)
    by_word = np.ascontiguousarray(scaled.reshape(k // 512, 128, 4, n).transpose(0, 1, 3, 2))
    if fmt == "e4m3":
        words = by_word.astype(ml_dtypes.float8_e4m3fn).view(np.uint8)
    else:
        c = by_word.astype(ml_dtypes.float4_e2m1fn).view(np.uint8) & 0xF
        words = (c[..., 0::2] | (c[..., 1::2] << 4)).reshape(k // 512, 128, 2 * n)
    return np.ascontiguousarray(words), np.ascontiguousarray(byte.astype(np.uint8).reshape(k // 512, 16, n))


def unpack_weight(words, scales, fmt):
    g, _, n = scales.shape
    words = np.ascontiguousarray(words).reshape(g, 128, n, -1)
    if fmt == "e4m3":
        vals = words.view(ml_dtypes.float8_e4m3fn).astype(np.float64)
    else:
        nib = np.empty((g, 128, n, 4), np.uint8)
        nib[..., 0::2] = words & 0xF
        nib[..., 1::2] = words >> 4
        vals = E2M1[nib]
    vals = vals * np.repeat(np.exp2(scales.astype(np.float64) - 127.0), 8, axis=1)[..., None]
    return vals.transpose(0, 1, 3, 2).reshape(g * 512, n)


D, E, T, I, Q = 512, 512, 2048, 512, 128


def setup_inputs():
    n = np.random.standard_normal
    idx = np.random.permutation(T)[:I]
    fd = mx_kscale(D)
    fe = mx_kscale(E)
    keysp = pack_weight(n((D, T)) / fd[:, None], "e4m3")
    valsp = pack_weight(n((E, T)) / fe[:, None], "e4m3")
    return {
        "query": (n((D, Q)) * 0.6 / np.sqrt(D) * fd[:, None]).astype(np.float32),
        "keys_words": keysp[0],
        "keys_scales": keysp[1],
        "z0": (np.random.uniform(200.0, 800.0, (Q, 1))).astype(np.float32),
        "c00": (np.random.uniform(-100.0, 100.0, (Q, 1))).astype(np.float32),
        "disc": (np.random.uniform(0.3, 1.0, (Q, 1))).astype(np.float32),
        "size": (np.random.uniform(0.5, 2.0, (1, I))).astype(np.float32),
        "gout": (n((E, Q)) * 1 / np.sqrt(E) * fe[:, None]).astype(np.float32),
        "vals_words": valsp[0],
        "vals_scales": valsp[1],
        "old": (0.5 * n((Q, T))).astype(np.float32),
        "offs": striped(idx),
    }


def reference(query, keys_words, keys_scales, z0, c00, disc, size, gout, vals_words, vals_scales, old, offs):
    idx = unstriped(offs)
    keysu = unpack_weight(keys_words, keys_scales, "e4m3")
    valsu = unpack_weight(vals_words, vals_scales, "e4m3")
    queryq = mxq(f64(query), 0, "e4m3")
    keysidxg = keysu[:, idx]
    a = queryq.T @ keysidxg
    p = np.exp(a)
    z = np.sum(p, axis=1, keepdims=True) + f64(z0) * f64(disc)
    goutq = mxq(f64(gout), 0, "e4m3")
    valsidxg = valsu[:, idx]
    c0 = goutq.T @ valsidxg
    dz = (np.sum(p * f64(size) * c0, axis=1, keepdims=True) + f64(c00) * f64(disc)) / np.square(z) * (-1.0)
    dp = 1.0 / z * c0 * f64(size) + dz
    da = dp * p
    gs = da * 512.0
    gf = np.zeros((Q, T))
    gf[:, idx] = gs
    y = f64(old) + gf
    return y

@@ -1,0 +1,164 @@
+from contextlib import ExitStack
+
+import concourse.mybir as mybir
+from concourse.masks import make_identity
+
+D, E, T, I, Q = 512, 512, 2048, 512, 128
+FLOPS = 2 * Q * I * (D + E)
+
+F32 = mybir.dt.float32
+BF16 = mybir.dt.bfloat16
+U32 = mybir.dt.uint32
+I32 = mybir.dt.int32
+U16 = mybir.dt.uint16
+U8 = mybir.dt.uint8
+FP8X4 = mybir.dt.float8_e4m3fn_x4
+ALU = mybir.AluOpType
+ACT = mybir.ActivationFunctionType
+
+P = 128
+PACK = 4
+HALF = I // 2
+VALS_ROW = 4
+OUT_CHUNKS = [512, 512, 512, 256, 256]
+
+
+def tile_attend_bresumed_s_kernel(tc, query, keys_words, keys_scales, z0, c00, disc, size, gout,
+                                   vals_words, vals_scales, old, offs, out):
+    nc = tc.nc
+    with ExitStack() as ctx:
+        sb = ctx.enter_context(tc.tile_pool(name="sb", bufs=1))
+        ps = ctx.enter_context(tc.psum_pool(name="ps", bufs=1))
+
+        offsets = sb.tile([P, I // 16], U16, name="offsets")
+        k_scale_pool = sb.tile([P, T], U8, name="k_scale_pool", align_bytes=64)
+        v_scale_pool = sb.tile([P, T], U8, name="v_scale_pool", align_bytes=64)
+        k_word_pool = sb.tile([P, T], I32, name="k_word_pool", align_bytes=64)
+        v_word_pool = sb.tile([P, T], I32, name="v_word_pool", align_bytes=64)
+        q_raw = sb.tile([P, PACK, Q], F32, name="q_raw")
+        g_raw = sb.tile([P, PACK, Q], F32, name="g_raw")
+        old_sb = sb.tile([P, T], F32, name="old_sb")
+        gf = sb.tile([P, T], F32, name="gf")
+        size_cols = sb.tile([P, PACK], F32, name="size_cols")
+        z0_sb = sb.tile([P, 1], F32, name="z0_sb")
+        c00_sb = sb.tile([P, 1], F32, name="c00_sb")
+        disc_sb = sb.tile([P, 1], F32, name="disc_sb")
+        ident = sb.tile([P, P], F32, name="ident")
+        warm = sb.tile([P, 1], F32, name="warm")
+        warm_out = sb.tile([P, 1], F32, name="warm_out")
+
+        nc.gpsimd.memset(k_scale_pool[:].bitcast(I32), 0)
+        nc.vector.memset(v_scale_pool[:].bitcast(I32), 0)
+        nc.vector.memset(warm[:], 0.0)
+        nc.scalar.activation(warm_out[:], warm[:], ACT.Exp)
+
+        def load_scales(queue, pool_tile, src, row0):
+            for quad in range(4):
+                queue.dma_start(
+                    out=pool_tile[32 * quad + row0: 32 * quad + row0 + 4, :].bitcast(I32),
+                    in_=src[0, 4 * quad: 4 * quad + 4, :].bitcast(I32))
+
+        nc.sync.dma_start(offsets[:], offs)
+        nc.sync.dma_start(out=size_cols[:], in_=size[0].rearrange("(n m) -> n m", m=PACK))
+        nc.sync.dma_start(out=q_raw[:], in_=query.rearrange("(p j) w -> p j w", j=PACK))
+        load_scales(nc.sync, k_scale_pool, keys_scales, 0)
+        nc.sync.dma_start(out=k_word_pool[:], in_=keys_words[0].rearrange("p n t -> p (n t)").bitcast(I32))
+        load_scales(nc.sync, v_scale_pool, vals_scales, VALS_ROW)
+        nc.sync.dma_start(out=g_raw[:], in_=gout.rearrange("(p j) w -> p j w", j=PACK))
+        nc.sync.dma_start(out=v_word_pool[:], in_=vals_words[0].rearrange("p n t -> p (n t)").bitcast(I32))
+        nc.sync.dma_start(out=old_sb[:], in_=old)
+        make_identity(nc, ident[:])
+        nc.gpsimd.dma_start(out=z0_sb[:], in_=z0)
+        nc.gpsimd.dma_start(out=disc_sb[:], in_=disc)
+        nc.gpsimd.dma_start(out=c00_sb[:], in_=c00)
+        nc.vector.memset(gf[:], 0.0)
+
+        size_ps = ps.tile([P, PACK, P], F32, name="size_ps")
+        for m in range(PACK):
+            nc.tensor.transpose(size_ps[:, m, :], size_cols[:, m:m + 1].to_broadcast([P, P]), ident[:])
+
+        def quantise(raw, name):
+            grouped = sb.tile([P, Q, PACK], BF16, name=name + "_grouped", align_bytes=64)
+            codes = sb.tile([P, Q], U32, name=name + "_codes", align_bytes=64)
+            scales = sb.tile([P, Q], U8, name=name + "_scales", align_bytes=64)
+            nc.scalar.copy(out=grouped[:].rearrange("p (c i) t -> p c t i", i=4),
+                           in_=raw[:].rearrange("p t (c i) -> p c t i", i=4))
+            nc.vector.quantize_mx(out=codes[:].bitcast(FP8X4), scales=scales[:],
+                                  in_=grouped[:].rearrange("p w j -> p (w j)"))
+            return codes, scales
+
+        def half_offsets(h):
+            return offsets[:, h * HALF // 16:(h + 1) * HALF // 16]
+
+        k_scales = sb.tile([P, I], U8, name="k_scales", align_bytes=64)
+        v_scales = sb.tile([P, I], U8, name="v_scales", align_bytes=64)
+        nc.vector.tensor_copy(k_scales[:], k_scale_pool[:].indirect(offsets[:]))
+        q_codes, q_scales = quantise(q_raw, "q")
+
+        p_sb = sb.tile([P, I], F32, name="p_sb")
+        p_sums = []
+        for h in range(2):
+            cols = slice(h * HALF, (h + 1) * HALF)
+            k_words = sb.tile([P, HALF], U32, name="k_words%d" % h, align_bytes=64)
+            nc.vector.tensor_copy(k_words[:], k_word_pool[:].bitcast(U32).indirect(half_offsets(h)))
+            a_ps = ps.tile([P, HALF], F32, name="a_ps%d" % h)
+            nc.tensor.matmul_mx(out=a_ps[:], lhsT=q_codes[:].bitcast(FP8X4), lhsT_scale=q_scales[:],
+                                rhs=k_words[:].bitcast(FP8X4), rhs_scale=k_scales[:, cols],
+                                start=True, stop=True)
+            p_sum = sb.tile([P, 1], F32, name="p_sum%d" % h)
+            nc.scalar.activation(p_sb[:, cols], a_ps[:], ACT.Exp, accum_out=p_sum[:])
+            p_sums.append(p_sum)
+
+        nc.vector.tensor_copy(v_scales[:], v_scale_pool[:].indirect(offsets[:]))
+        g_codes, g_scales = quantise(g_raw, "g")
+
+        z = sb.tile([P, 1], F32, name="z")
+        r = sb.tile([P, 1], F32, name="r")
+        zd = sb.tile([P, 1], F32, name="zd")
+        cd = sb.tile([P, 1], F32, name="cd")
+        nc.gpsimd.tensor_tensor(zd[:], z0_sb[:], disc_sb[:], ALU.mult)
+        nc.gpsimd.tensor_scalar(cd[:], c00_sb[:], disc_sb[:], 512.0, ALU.mult, ALU.mult)
+        p_size = sb.tile([P, I], F32, name="p_size")
+        nc.vector.tensor_scalar(z[:], p_sums[0][:], zd[:], p_sums[1][:], ALU.add, ALU.add)
+        nc.vector.scalar_tensor_tensor(
+            p_size[:].rearrange("p (n m) -> p n m", m=PACK), p_sb[:].rearrange("p (n m) -> p n m", m=PACK),
+            512.0, size_ps[:].rearrange("p m n -> p n m"), ALU.mult, ALU.mult)
+        nc.vector.reciprocal(r[:], z[:])
+
+        c_banks = []
+        for h in range(2):
+            cols = slice(h * HALF, (h + 1) * HALF)
+            v_words = sb.tile([P, HALF], U32, name="v_words%d" % h, align_bytes=64)
+            nc.vector.tensor_copy(v_words[:], v_word_pool[:].bitcast(U32).indirect(half_offsets(h)))
+            c_ps = ps.tile([P, HALF], F32, name="c_ps%d" % h)
+            nc.tensor.matmul_mx(out=c_ps[:], lhsT=g_codes[:].bitcast(FP8X4), lhsT_scale=g_scales[:],
+                                rhs=v_words[:].bitcast(FP8X4), rhs_scale=v_scales[VALS_ROW:, cols],
+                                start=True, stop=True)
+            c_banks.append(c_ps)
+
+        direct = sb.tile([P, I], F32, name="direct")
+        sums = []
+        for h in range(2):
+            cols = slice(h * HALF, (h + 1) * HALF)
+            s = sb.tile([P, 1], F32, name="direct_sum%d" % h)
+            nc.vector.scalar_tensor_tensor(direct[:, cols], c_banks[h][:], r[:], p_size[:, cols],
+                                           ALU.mult, ALU.mult, accum_out=s[:])
+            sums.append(s)
+            if h == 0:
+                carry2 = sb.tile([P, 1], F32, name="carry2")
+                nc.vector.tensor_scalar(carry2[:], cd[:], r[:], s[:], ALU.mult, ALU.add)
+
+        dz = sb.tile([P, 1], F32, name="dz")
+        nc.vector.tensor_scalar(dz[:], sums[1][:], carry2[:], r[:], ALU.add, ALU.mult)
+        through_z = sb.tile([P, I], F32, name="through_z")
+        nc.vector.tensor_scalar(through_z[:], p_sb[:], dz[:], -1.0, ALU.mult, ALU.mult)
+        nc.vector.tensor_tensor(gf[:].indirect(offsets[:]), direct[:], through_z[:], ALU.add)
+
+        start = 0
+        for c, width in enumerate(OUT_CHUNKS):
+            cols = slice(start, start + width)
+            res = sb.tile([P, width], F32, name="res%d" % c)
+            nc.vector.tensor_tensor(res[:], gf[:, cols], old_sb[:, cols], ALU.add)
+            queue = nc.sync if c % 2 == 0 else nc.scalar
+            queue.dma_start(out=out[:, cols], in_=res[:])
+            start += width

@@ -20,7 +20,7 @@ P = 128
 PACK = 4
 HALF = I // 2
 VALS_ROW = 4
-OUT_CHUNKS = [512, 512, 512, 256, 256]
+OUT_CHUNKS = [256, 512, 512, 512, 256]
 
 
 def tile_attend_bresumed_s_kernel(tc, query, keys_words, keys_scales, z0, c00, disc, size, gout,
@@ -34,7 +34,7 @@ def tile_attend_bresumed_s_kernel(tc, query, keys_words, keys_scales, z0, c00, d
         k_scale_pool = sb.tile([P, T], U8, name="k_scale_pool", align_bytes=64)
         v_scale_pool = sb.tile([P, T], U8, name="v_scale_pool", align_bytes=64)
         k_word_pool = sb.tile([P, T], I32, name="k_word_pool", align_bytes=64)
-        v_word_pool = sb.tile([P, T], I32, name="v_word_pool", align_bytes=64)
+        v_word_pool = sb.tile([P, T], I32, name="v_word_pool", tag="v_word_pool", align_bytes=64)
         q_raw = sb.tile([P, PACK, Q], F32, name="q_raw")
         g_raw = sb.tile([P, PACK, Q], F32, name="g_raw")
         old_sb = sb.tile([P, T], F32, name="old_sb")
@@ -48,44 +48,39 @@ def tile_attend_bresumed_s_kernel(tc, query, keys_words, keys_scales, z0, c00, d
         warm_out = sb.tile([P, 1], F32, name="warm_out")
 
         nc.gpsimd.memset(k_scale_pool[:].bitcast(I32), 0)
+        make_identity(nc, ident[:])
         nc.vector.memset(v_scale_pool[:].bitcast(I32), 0)
+        nc.gpsimd.memset(gf[:].bitcast(I32), 0)
         nc.vector.memset(warm[:], 0.0)
         nc.scalar.activation(warm_out[:], warm[:], ACT.Exp)
 
         def load_scales(queue, pool_tile, src, row0):
-            for quad in range(4):
+            for j in range(4):
                 queue.dma_start(
-                    out=pool_tile[32 * quad + row0: 32 * quad + row0 + 4, :].bitcast(I32),
-                    in_=src[0, 4 * quad: 4 * quad + 4, :].bitcast(I32))
+                    out=pool_tile[row0 + j: P: 32, :].bitcast(I32),
+                    in_=src[0, j: 16: 4, :].bitcast(I32))
 
         nc.sync.dma_start(offsets[:], offs)
-        nc.sync.dma_start(out=size_cols[:], in_=size[0].rearrange("(n m) -> n m", m=PACK))
         nc.sync.dma_start(out=q_raw[:], in_=query.rearrange("(p j) w -> p j w", j=PACK))
+        nc.sync.dma_start(out=g_raw[:], in_=gout.rearrange("(p j) w -> p j w", j=PACK))
         load_scales(nc.sync, k_scale_pool, keys_scales, 0)
         nc.sync.dma_start(out=k_word_pool[:], in_=keys_words[0].rearrange("p n t -> p (n t)").bitcast(I32))
         load_scales(nc.sync, v_scale_pool, vals_scales, VALS_ROW)
-        nc.sync.dma_start(out=g_raw[:], in_=gout.rearrange("(p j) w -> p j w", j=PACK))
+        nc.sync.dma_start(out=size_cols[:], in_=size[0].rearrange("(n m) -> n m", m=PACK))
+        nc.sync.dma_start(out=z0_sb[:], in_=z0)
         nc.sync.dma_start(out=v_word_pool[:], in_=vals_words[0].rearrange("p n t -> p (n t)").bitcast(I32))
+        nc.sync.dma_start(out=disc_sb[:], in_=disc)
+        nc.sync.dma_start(out=c00_sb[:], in_=c00)
         nc.sync.dma_start(out=old_sb[:], in_=old)
-        make_identity(nc, ident[:])
-        nc.gpsimd.dma_start(out=z0_sb[:], in_=z0)
-        nc.gpsimd.dma_start(out=disc_sb[:], in_=disc)
-        nc.gpsimd.dma_start(out=c00_sb[:], in_=c00)
-        nc.vector.memset(gf[:], 0.0)
 
-        size_ps = ps.tile([P, PACK, P], F32, name="size_ps")
-        for m in range(PACK):
-            nc.tensor.transpose(size_ps[:, m, :], size_cols[:, m:m + 1].to_broadcast([P, P]), ident[:])
-
-        def quantise(raw, name):
-            grouped = sb.tile([P, Q, PACK], BF16, name=name + "_grouped", align_bytes=64)
-            codes = sb.tile([P, Q], U32, name=name + "_codes", align_bytes=64)
-            scales = sb.tile([P, Q], U8, name=name + "_scales", align_bytes=64)
-            nc.scalar.copy(out=grouped[:].rearrange("p (c i) t -> p c t i", i=4),
+        grouped = sb.tile([P, 2, Q, PACK], BF16, name="grouped", align_bytes=64)
+        row_codes = sb.tile([P, 2 * Q], U32, name="row_codes", align_bytes=64)
+        row_scales = sb.tile([P, 2 * Q], U8, name="row_scales", align_bytes=64)
+        for n, raw in enumerate((q_raw, g_raw)):
+            nc.scalar.copy(out=grouped[:, n].rearrange("p (c i) t -> p c t i", i=4),
                            in_=raw[:].rearrange("p t (c i) -> p c t i", i=4))
-            nc.vector.quantize_mx(out=codes[:].bitcast(FP8X4), scales=scales[:],
-                                  in_=grouped[:].rearrange("p w j -> p (w j)"))
-            return codes, scales
+        q_codes, g_codes = row_codes[:, 0:Q], row_codes[:, Q:2 * Q]
+        q_scales, g_scales = row_scales[:, 0:Q], row_scales[:, Q:2 * Q]
 
         def half_offsets(h):
             return offsets[:, h * HALF // 16:(h + 1) * HALF // 16]
@@ -93,16 +88,17 @@ def tile_attend_bresumed_s_kernel(tc, query, keys_words, keys_scales, z0, c00, d
         k_scales = sb.tile([P, I], U8, name="k_scales", align_bytes=64)
         v_scales = sb.tile([P, I], U8, name="v_scales", align_bytes=64)
         nc.vector.tensor_copy(k_scales[:], k_scale_pool[:].indirect(offsets[:]))
-        q_codes, q_scales = quantise(q_raw, "q")
+        nc.vector.quantize_mx(out=row_codes[:].bitcast(FP8X4), scales=row_scales[:],
+                              in_=grouped[:].rearrange("p n w j -> p (n w j)"))
 
         p_sb = sb.tile([P, I], F32, name="p_sb")
         p_sums = []
         for h in range(2):
             cols = slice(h * HALF, (h + 1) * HALF)
-            k_words = sb.tile([P, HALF], U32, name="k_words%d" % h, align_bytes=64)
+            k_words = sb.tile([P, HALF], U32, name="k_words%d" % h, tag="k_words%d" % h, align_bytes=64)
             nc.vector.tensor_copy(k_words[:], k_word_pool[:].bitcast(U32).indirect(half_offsets(h)))
             a_ps = ps.tile([P, HALF], F32, name="a_ps%d" % h)
-            nc.tensor.matmul_mx(out=a_ps[:], lhsT=q_codes[:].bitcast(FP8X4), lhsT_scale=q_scales[:],
+            nc.tensor.matmul_mx(out=a_ps[:], lhsT=q_codes.bitcast(FP8X4), lhsT_scale=q_scales,
                                 rhs=k_words[:].bitcast(FP8X4), rhs_scale=k_scales[:, cols],
                                 start=True, stop=True)
             p_sum = sb.tile([P, 1], F32, name="p_sum%d" % h)
@@ -110,20 +106,16 @@ def tile_attend_bresumed_s_kernel(tc, query, keys_words, keys_scales, z0, c00, d
             p_sums.append(p_sum)
 
         nc.vector.tensor_copy(v_scales[:], v_scale_pool[:].indirect(offsets[:]))
-        g_codes, g_scales = quantise(g_raw, "g")
 
-        z = sb.tile([P, 1], F32, name="z")
-        r = sb.tile([P, 1], F32, name="r")
-        zd = sb.tile([P, 1], F32, name="zd")
-        cd = sb.tile([P, 1], F32, name="cd")
-        nc.gpsimd.tensor_tensor(zd[:], z0_sb[:], disc_sb[:], ALU.mult)
-        nc.gpsimd.tensor_scalar(cd[:], c00_sb[:], disc_sb[:], 512.0, ALU.mult, ALU.mult)
+        size_ps = ps.tile([P, PACK, P], F32, name="size_ps")
+        for m in range(PACK):
+            nc.tensor.transpose(size_ps[:, m, :], size_cols[:, m:m + 1].to_broadcast([P, P]), ident[:])
+
+
         p_size = sb.tile([P, I], F32, name="p_size")
-        nc.vector.tensor_scalar(z[:], p_sums[0][:], zd[:], p_sums[1][:], ALU.add, ALU.add)
         nc.vector.scalar_tensor_tensor(
             p_size[:].rearrange("p (n m) -> p n m", m=PACK), p_sb[:].rearrange("p (n m) -> p n m", m=PACK),
             512.0, size_ps[:].rearrange("p m n -> p n m"), ALU.mult, ALU.mult)
-        nc.vector.reciprocal(r[:], z[:])
 
         c_banks = []
         for h in range(2):
@@ -131,10 +123,19 @@ def tile_attend_bresumed_s_kernel(tc, query, keys_words, keys_scales, z0, c00, d
             v_words = sb.tile([P, HALF], U32, name="v_words%d" % h, align_bytes=64)
             nc.vector.tensor_copy(v_words[:], v_word_pool[:].bitcast(U32).indirect(half_offsets(h)))
             c_ps = ps.tile([P, HALF], F32, name="c_ps%d" % h)
-            nc.tensor.matmul_mx(out=c_ps[:], lhsT=g_codes[:].bitcast(FP8X4), lhsT_scale=g_scales[:],
+            nc.tensor.matmul_mx(out=c_ps[:], lhsT=g_codes.bitcast(FP8X4), lhsT_scale=g_scales,
                                 rhs=v_words[:].bitcast(FP8X4), rhs_scale=v_scales[VALS_ROW:, cols],
                                 start=True, stop=True)
             c_banks.append(c_ps)
+
+        p_total = sb.tile([P, 1], F32, name="p_total")
+        z = sb.tile([P, 1], F32, name="z")
+        r = sb.tile([P, 1], F32, name="r", tag="v_word_pool", align_bytes=64)
+        cd = sb.tile([P, 1], F32, name="cd")
+        nc.scalar.activation(p_total[:], p_sums[0][:], ACT.Identity, bias=p_sums[1][:])
+        nc.scalar.activation(z[:], z0_sb[:], ACT.Identity, bias=p_total[:], scale=disc_sb[:])
+        nc.gpsimd.tensor_scalar(cd[:], c00_sb[:], disc_sb[:], 512.0, ALU.mult, ALU.mult)
+        nc.vector.reciprocal(r[:], z[:])
 
         direct = sb.tile([P, I], F32, name="direct")
         sums = []

@@ -18,9 +18,12 @@ ACT = mybir.ActivationFunctionType
 
 P = 128
 PACK = 4
-HALF = I // 2
-VALS_ROW = 4
-OUT_CHUNKS = [256, 512, 512, 512, 256]
+QUADRANT = 32
+BLOCKS = D // 32
+LINE = 4
+GS_FACTOR = 512.0
+VALS_SCALE_ROW = 4
+OUT_WIDTHS = [256, 512, 512, 512, 256]
 
 
 def tile_attend_bresumed_s_kernel(tc, query, keys_words, keys_scales, z0, c00, disc, size, gout,
@@ -44,28 +47,23 @@ def tile_attend_bresumed_s_kernel(tc, query, keys_words, keys_scales, z0, c00, d
         c00_sb = sb.tile([P, 1], F32, name="c00_sb")
         disc_sb = sb.tile([P, 1], F32, name="disc_sb")
         ident = sb.tile([P, P], F32, name="ident")
-        warm = sb.tile([P, 1], F32, name="warm")
-        warm_out = sb.tile([P, 1], F32, name="warm_out")
 
         nc.gpsimd.memset(k_scale_pool[:].bitcast(I32), 0)
         make_identity(nc, ident[:])
         nc.vector.memset(v_scale_pool[:].bitcast(I32), 0)
         nc.gpsimd.memset(gf[:].bitcast(I32), 0)
-        nc.vector.memset(warm[:], 0.0)
-        nc.scalar.activation(warm_out[:], warm[:], ACT.Exp)
 
-        def load_scales(queue, pool_tile, src, row0):
+        def load_scale_rows(pool_tile, scales, first_row):
             for j in range(4):
-                queue.dma_start(
-                    out=pool_tile[row0 + j: P: 32, :].bitcast(I32),
-                    in_=src[0, j: 16: 4, :].bitcast(I32))
+                nc.sync.dma_start(out=pool_tile[first_row + j:P:QUADRANT, :].bitcast(I32),
+                                  in_=scales[0, j:BLOCKS:4, :].bitcast(I32))
 
         nc.sync.dma_start(offsets[:], offs)
         nc.sync.dma_start(out=q_raw[:], in_=query.rearrange("(p j) w -> p j w", j=PACK))
         nc.sync.dma_start(out=g_raw[:], in_=gout.rearrange("(p j) w -> p j w", j=PACK))
-        load_scales(nc.sync, k_scale_pool, keys_scales, 0)
+        load_scale_rows(k_scale_pool, keys_scales, 0)
         nc.sync.dma_start(out=k_word_pool[:], in_=keys_words[0].rearrange("p n t -> p (n t)").bitcast(I32))
-        load_scales(nc.sync, v_scale_pool, vals_scales, VALS_ROW)
+        load_scale_rows(v_scale_pool, vals_scales, VALS_SCALE_ROW)
         nc.sync.dma_start(out=size_cols[:], in_=size[0].rearrange("(n m) -> n m", m=PACK))
         nc.sync.dma_start(out=z0_sb[:], in_=z0)
         nc.sync.dma_start(out=v_word_pool[:], in_=vals_words[0].rearrange("p n t -> p (n t)").bitcast(I32))
@@ -77,13 +75,10 @@ def tile_attend_bresumed_s_kernel(tc, query, keys_words, keys_scales, z0, c00, d
         row_codes = sb.tile([P, 2 * Q], U32, name="row_codes", align_bytes=64)
         row_scales = sb.tile([P, 2 * Q], U8, name="row_scales", align_bytes=64)
         for n, raw in enumerate((q_raw, g_raw)):
-            nc.scalar.copy(out=grouped[:, n].rearrange("p (c i) t -> p c t i", i=4),
-                           in_=raw[:].rearrange("p t (c i) -> p c t i", i=4))
+            nc.scalar.copy(out=grouped[:, n].rearrange("p (c i) t -> p c t i", i=LINE),
+                           in_=raw[:].rearrange("p t (c i) -> p c t i", i=LINE))
         q_codes, g_codes = row_codes[:, 0:Q], row_codes[:, Q:2 * Q]
         q_scales, g_scales = row_scales[:, 0:Q], row_scales[:, Q:2 * Q]
-
-        def half_offsets(h):
-            return offsets[:, h * HALF // 16:(h + 1) * HALF // 16]
 
         k_scales = sb.tile([P, I], U8, name="k_scales", align_bytes=64)
         v_scales = sb.tile([P, I], U8, name="v_scales", align_bytes=64)
@@ -92,18 +87,13 @@ def tile_attend_bresumed_s_kernel(tc, query, keys_words, keys_scales, z0, c00, d
                               in_=grouped[:].rearrange("p n w j -> p (n w j)"))
 
         p_sb = sb.tile([P, I], F32, name="p_sb")
-        p_sums = []
-        for h in range(2):
-            cols = slice(h * HALF, (h + 1) * HALF)
-            k_words = sb.tile([P, HALF], U32, name="k_words%d" % h, tag="k_words%d" % h, align_bytes=64)
-            nc.vector.tensor_copy(k_words[:], k_word_pool[:].bitcast(U32).indirect(half_offsets(h)))
-            a_ps = ps.tile([P, HALF], F32, name="a_ps%d" % h)
-            nc.tensor.matmul_mx(out=a_ps[:], lhsT=q_codes.bitcast(FP8X4), lhsT_scale=q_scales,
-                                rhs=k_words[:].bitcast(FP8X4), rhs_scale=k_scales[:, cols],
-                                start=True, stop=True)
-            p_sum = sb.tile([P, 1], F32, name="p_sum%d" % h)
-            nc.scalar.activation(p_sb[:, cols], a_ps[:], ACT.Exp, accum_out=p_sum[:])
-            p_sums.append(p_sum)
+        p_sum = sb.tile([P, 1], F32, name="p_sum")
+        k_words = sb.tile([P, I], U32, name="k_words", align_bytes=64)
+        nc.vector.tensor_copy(k_words[:], k_word_pool[:].bitcast(U32).indirect(offsets[:]))
+        a_ps = ps.tile([P, I], F32, name="a_ps")
+        nc.tensor.matmul_mx(out=a_ps[:], lhsT=q_codes.bitcast(FP8X4), lhsT_scale=q_scales,
+                            rhs=k_words[:].bitcast(FP8X4), rhs_scale=k_scales[:], start=True, stop=True)
+        nc.scalar.activation(p_sb[:], a_ps[:], ACT.Exp, accum_out=p_sum[:])
 
         nc.vector.tensor_copy(v_scales[:], v_scale_pool[:].indirect(offsets[:]))
 
@@ -111,55 +101,41 @@ def tile_attend_bresumed_s_kernel(tc, query, keys_words, keys_scales, z0, c00, d
         for m in range(PACK):
             nc.tensor.transpose(size_ps[:, m, :], size_cols[:, m:m + 1].to_broadcast([P, P]), ident[:])
 
+        v_words = sb.tile([P, I], U32, name="v_words", align_bytes=64)
+        nc.vector.tensor_copy(v_words[:], v_word_pool[:].bitcast(U32).indirect(offsets[:]))
+        c_ps = ps.tile([P, I], F32, name="c_ps")
+        nc.tensor.matmul_mx(out=c_ps[:], lhsT=g_codes.bitcast(FP8X4), lhsT_scale=g_scales,
+                            rhs=v_words[:].bitcast(FP8X4), rhs_scale=v_scales[VALS_SCALE_ROW:, :],
+                            start=True, stop=True)
 
-        p_size = sb.tile([P, I], F32, name="p_size")
+        z = sb.tile([P, 1], F32, name="z")
+        r = sb.tile([P, 1], F32, name="r")
+        c00_disc = sb.tile([P, 1], F32, name="c00_disc")
+        carry = sb.tile([P, 1], F32, name="carry")
+        nc.scalar.activation(z[:], z0_sb[:], ACT.Identity, bias=p_sum[:], scale=disc_sb[:])
+        nc.gpsimd.tensor_scalar(c00_disc[:], c00_sb[:], disc_sb[:], GS_FACTOR, ALU.mult, ALU.mult)
+        nc.vector.reciprocal(r[:], z[:])
+        p_size = sb.tile([P, I], F32, name="p_size", tag="v_word_pool", align_bytes=64)
         nc.vector.scalar_tensor_tensor(
             p_size[:].rearrange("p (n m) -> p n m", m=PACK), p_sb[:].rearrange("p (n m) -> p n m", m=PACK),
-            512.0, size_ps[:].rearrange("p m n -> p n m"), ALU.mult, ALU.mult)
-
-        c_banks = []
-        for h in range(2):
-            cols = slice(h * HALF, (h + 1) * HALF)
-            v_words = sb.tile([P, HALF], U32, name="v_words%d" % h, align_bytes=64)
-            nc.vector.tensor_copy(v_words[:], v_word_pool[:].bitcast(U32).indirect(half_offsets(h)))
-            c_ps = ps.tile([P, HALF], F32, name="c_ps%d" % h)
-            nc.tensor.matmul_mx(out=c_ps[:], lhsT=g_codes.bitcast(FP8X4), lhsT_scale=g_scales,
-                                rhs=v_words[:].bitcast(FP8X4), rhs_scale=v_scales[VALS_ROW:, cols],
-                                start=True, stop=True)
-            c_banks.append(c_ps)
-
-        p_total = sb.tile([P, 1], F32, name="p_total")
-        z = sb.tile([P, 1], F32, name="z")
-        r = sb.tile([P, 1], F32, name="r", tag="v_word_pool", align_bytes=64)
-        cd = sb.tile([P, 1], F32, name="cd")
-        nc.scalar.activation(p_total[:], p_sums[0][:], ACT.Identity, bias=p_sums[1][:])
-        nc.scalar.activation(z[:], z0_sb[:], ACT.Identity, bias=p_total[:], scale=disc_sb[:])
-        nc.gpsimd.tensor_scalar(cd[:], c00_sb[:], disc_sb[:], 512.0, ALU.mult, ALU.mult)
-        nc.vector.reciprocal(r[:], z[:])
+            GS_FACTOR, size_ps[:].rearrange("p m n -> p n m"), ALU.mult, ALU.mult)
+        nc.scalar.mul(carry[:], c00_disc[:], r[:])
 
         direct = sb.tile([P, I], F32, name="direct")
-        sums = []
-        for h in range(2):
-            cols = slice(h * HALF, (h + 1) * HALF)
-            s = sb.tile([P, 1], F32, name="direct_sum%d" % h)
-            nc.vector.scalar_tensor_tensor(direct[:, cols], c_banks[h][:], r[:], p_size[:, cols],
-                                           ALU.mult, ALU.mult, accum_out=s[:])
-            sums.append(s)
-            if h == 0:
-                carry2 = sb.tile([P, 1], F32, name="carry2")
-                nc.vector.tensor_scalar(carry2[:], cd[:], r[:], s[:], ALU.mult, ALU.add)
-
+        direct_sum = sb.tile([P, 1], F32, name="direct_sum")
+        nc.vector.scalar_tensor_tensor(direct[:], c_ps[:], r[:], p_size[:], ALU.mult, ALU.mult,
+                                       accum_out=direct_sum[:])
         dz = sb.tile([P, 1], F32, name="dz")
-        nc.vector.tensor_scalar(dz[:], sums[1][:], carry2[:], r[:], ALU.add, ALU.mult)
+        nc.vector.tensor_scalar(dz[:], direct_sum[:], carry[:], r[:], ALU.add, ALU.mult)
         through_z = sb.tile([P, I], F32, name="through_z")
         nc.vector.tensor_scalar(through_z[:], p_sb[:], dz[:], -1.0, ALU.mult, ALU.mult)
         nc.vector.tensor_tensor(gf[:].indirect(offsets[:]), direct[:], through_z[:], ALU.add)
 
-        start = 0
-        for c, width in enumerate(OUT_CHUNKS):
-            cols = slice(start, start + width)
-            res = sb.tile([P, width], F32, name="res%d" % c)
-            nc.vector.tensor_tensor(res[:], gf[:, cols], old_sb[:, cols], ALU.add)
+        first = 0
+        for c, width in enumerate(OUT_WIDTHS):
+            cols = slice(first, first + width)
+            result = sb.tile([P, width], F32, name="result%d" % c)
+            nc.vector.tensor_tensor(result[:], gf[:, cols], old_sb[:, cols], ALU.add)
             queue = nc.sync if c % 2 == 0 else nc.scalar
-            queue.dma_start(out=out[:, cols], in_=res[:])
-            start += width
+            queue.dma_start(out=out[:, cols], in_=result[:])
+            first += width

from contextlib import ExitStack

import concourse.mybir as mybir
from concourse.masks import make_identity

D, E, T, I, Q = 512, 512, 2048, 512, 128
FLOPS = 2 * Q * I * (D + E)

F32 = mybir.dt.float32
BF16 = mybir.dt.bfloat16
U32 = mybir.dt.uint32
I32 = mybir.dt.int32
U16 = mybir.dt.uint16
U8 = mybir.dt.uint8
FP8X4 = mybir.dt.float8_e4m3fn_x4
ALU = mybir.AluOpType
ACT = mybir.ActivationFunctionType

P = 128
PACK = 4
QUADRANT = 32
BLOCKS = D // 32
LINE = 4
GS_FACTOR = 512.0
VALS_SCALE_ROW = 4
OUT_WIDTHS = [256, 512, 512, 512, 256]


def tile_attend_bresumed_s_kernel(tc, query, keys_words, keys_scales, z0, c00, disc, size, gout,
                                   vals_words, vals_scales, old, offs, out):
    nc = tc.nc
    with ExitStack() as ctx:
        sb = ctx.enter_context(tc.tile_pool(name="sb", bufs=1))
        ps = ctx.enter_context(tc.psum_pool(name="ps", bufs=1))

        offsets = sb.tile([P, I // 16], U16, name="offsets")
        k_scale_pool = sb.tile([P, T], U8, name="k_scale_pool", align_bytes=64)
        v_scale_pool = sb.tile([P, T], U8, name="v_scale_pool", align_bytes=64)
        k_word_pool = sb.tile([P, T], I32, name="k_word_pool", align_bytes=64)
        v_word_pool = sb.tile([P, T], I32, name="v_word_pool", tag="v_word_pool", align_bytes=64)
        q_raw = sb.tile([P, PACK, Q], F32, name="q_raw")
        g_raw = sb.tile([P, PACK, Q], F32, name="g_raw")
        old_sb = sb.tile([P, T], F32, name="old_sb")
        gf = sb.tile([P, T], F32, name="gf")
        size_cols = sb.tile([P, PACK], F32, name="size_cols")
        z0_sb = sb.tile([P, 1], F32, name="z0_sb")
        c00_sb = sb.tile([P, 1], F32, name="c00_sb")
        disc_sb = sb.tile([P, 1], F32, name="disc_sb")
        ident = sb.tile([P, P], F32, name="ident")

        nc.gpsimd.memset(k_scale_pool[:].bitcast(I32), 0)
        make_identity(nc, ident[:])
        nc.vector.memset(v_scale_pool[:].bitcast(I32), 0)
        nc.gpsimd.memset(gf[:].bitcast(I32), 0)

        def load_scale_rows(pool_tile, scales, first_row):
            for j in range(4):
                nc.sync.dma_start(out=pool_tile[first_row + j:P:QUADRANT, :].bitcast(I32),
                                  in_=scales[0, j:BLOCKS:4, :].bitcast(I32))

        nc.sync.dma_start(offsets[:], offs)
        nc.sync.dma_start(out=q_raw[:], in_=query.rearrange("(p j) w -> p j w", j=PACK))
        nc.sync.dma_start(out=g_raw[:], in_=gout.rearrange("(p j) w -> p j w", j=PACK))
        load_scale_rows(k_scale_pool, keys_scales, 0)
        nc.sync.dma_start(out=k_word_pool[:], in_=keys_words[0].rearrange("p n t -> p (n t)").bitcast(I32))
        load_scale_rows(v_scale_pool, vals_scales, VALS_SCALE_ROW)
        nc.sync.dma_start(out=size_cols[:], in_=size[0].rearrange("(n m) -> n m", m=PACK))
        nc.sync.dma_start(out=z0_sb[:], in_=z0)
        nc.sync.dma_start(out=v_word_pool[:], in_=vals_words[0].rearrange("p n t -> p (n t)").bitcast(I32))
        nc.sync.dma_start(out=disc_sb[:], in_=disc)
        nc.sync.dma_start(out=c00_sb[:], in_=c00)
        nc.sync.dma_start(out=old_sb[:], in_=old)

        grouped = sb.tile([P, 2, Q, PACK], BF16, name="grouped", align_bytes=64)
        row_codes = sb.tile([P, 2 * Q], U32, name="row_codes", align_bytes=64)
        row_scales = sb.tile([P, 2 * Q], U8, name="row_scales", align_bytes=64)
        for n, raw in enumerate((q_raw, g_raw)):
            nc.scalar.copy(out=grouped[:, n].rearrange("p (c i) t -> p c t i", i=LINE),
                           in_=raw[:].rearrange("p t (c i) -> p c t i", i=LINE))
        q_codes, g_codes = row_codes[:, 0:Q], row_codes[:, Q:2 * Q]
        q_scales, g_scales = row_scales[:, 0:Q], row_scales[:, Q:2 * Q]

        k_scales = sb.tile([P, I], U8, name="k_scales", align_bytes=64)
        v_scales = sb.tile([P, I], U8, name="v_scales", align_bytes=64)
        nc.vector.tensor_copy(k_scales[:], k_scale_pool[:].indirect(offsets[:]))
        nc.vector.quantize_mx(out=row_codes[:].bitcast(FP8X4), scales=row_scales[:],
                              in_=grouped[:].rearrange("p n w j -> p (n w j)"))

        p_sb = sb.tile([P, I], F32, name="p_sb")
        p_sum = sb.tile([P, 1], F32, name="p_sum")
        k_words = sb.tile([P, I], U32, name="k_words", align_bytes=64)
        nc.vector.tensor_copy(k_words[:], k_word_pool[:].bitcast(U32).indirect(offsets[:]))
        a_ps = ps.tile([P, I], F32, name="a_ps")
        nc.tensor.matmul_mx(out=a_ps[:], lhsT=q_codes.bitcast(FP8X4), lhsT_scale=q_scales,
                            rhs=k_words[:].bitcast(FP8X4), rhs_scale=k_scales[:], start=True, stop=True)
        nc.scalar.activation(p_sb[:], a_ps[:], ACT.Exp, accum_out=p_sum[:])

        nc.vector.tensor_copy(v_scales[:], v_scale_pool[:].indirect(offsets[:]))

        size_ps = ps.tile([P, PACK, P], F32, name="size_ps")
        for m in range(PACK):
            nc.tensor.transpose(size_ps[:, m, :], size_cols[:, m:m + 1].to_broadcast([P, P]), ident[:])

        v_words = sb.tile([P, I], U32, name="v_words", align_bytes=64)
        nc.vector.tensor_copy(v_words[:], v_word_pool[:].bitcast(U32).indirect(offsets[:]))
        c_ps = ps.tile([P, I], F32, name="c_ps")
        nc.tensor.matmul_mx(out=c_ps[:], lhsT=g_codes.bitcast(FP8X4), lhsT_scale=g_scales,
                            rhs=v_words[:].bitcast(FP8X4), rhs_scale=v_scales[VALS_SCALE_ROW:, :],
                            start=True, stop=True)

        z = sb.tile([P, 1], F32, name="z")
        r = sb.tile([P, 1], F32, name="r")
        c00_disc = sb.tile([P, 1], F32, name="c00_disc")
        carry = sb.tile([P, 1], F32, name="carry")
        nc.scalar.activation(z[:], z0_sb[:], ACT.Identity, bias=p_sum[:], scale=disc_sb[:])
        nc.gpsimd.tensor_scalar(c00_disc[:], c00_sb[:], disc_sb[:], GS_FACTOR, ALU.mult, ALU.mult)
        nc.vector.reciprocal(r[:], z[:])
        p_size = sb.tile([P, I], F32, name="p_size", tag="v_word_pool", align_bytes=64)
        nc.vector.scalar_tensor_tensor(
            p_size[:].rearrange("p (n m) -> p n m", m=PACK), p_sb[:].rearrange("p (n m) -> p n m", m=PACK),
            GS_FACTOR, size_ps[:].rearrange("p m n -> p n m"), ALU.mult, ALU.mult)
        nc.scalar.mul(carry[:], c00_disc[:], r[:])

        direct = sb.tile([P, I], F32, name="direct")
        direct_sum = sb.tile([P, 1], F32, name="direct_sum")
        nc.vector.scalar_tensor_tensor(direct[:], c_ps[:], r[:], p_size[:], ALU.mult, ALU.mult,
                                       accum_out=direct_sum[:])
        dz = sb.tile([P, 1], F32, name="dz")
        nc.vector.tensor_scalar(dz[:], direct_sum[:], carry[:], r[:], ALU.add, ALU.mult)
        through_z = sb.tile([P, I], F32, name="through_z")
        nc.vector.tensor_scalar(through_z[:], p_sb[:], dz[:], -1.0, ALU.mult, ALU.mult)
        nc.vector.tensor_tensor(gf[:].indirect(offsets[:]), direct[:], through_z[:], ALU.add)

        first = 0
        for c, width in enumerate(OUT_WIDTHS):
            cols = slice(first, first + width)
            result = sb.tile([P, width], F32, name="result%d" % c)
            nc.vector.tensor_tensor(result[:], gf[:, cols], old_sb[:, cols], ALU.add)
            queue = nc.sync if c % 2 == 0 else nc.scalar
            queue.dma_start(out=out[:, cols], in_=result[:])
            first += width
